import numpy as np
import ml_dtypes


def mxq(x, axis, fmt="e4m3"):
    dtype, down = {"e4m3": (ml_dtypes.float8_e4m3fn, 7), "e5m2": (ml_dtypes.float8_e5m2, 14)}[fmt]
    v = np.moveaxis(np.asarray(x, np.float32).astype(ml_dtypes.bfloat16).astype(np.float64), axis, -1)
    blocks = v.reshape(v.shape[:-1] + (-1, 32))
    amax = np.abs(blocks).max(-1, keepdims=True)
    byte = np.maximum(np.where(amax > 0, np.frexp(amax)[1] - 1 + 127, 0) - down, 1)
    scale = np.exp2(byte - 127.0)
    codes = (blocks / scale).astype(np.float32).astype(dtype).astype(np.float64)
    return np.moveaxis((codes * scale).reshape(v.shape), -1, axis)


WIDE = False


def mx_kscale(k):
    if not WIDE:
        return np.ones(k)
    levels = np.array([10, -10, 5, -5, 0])
    if k % 512:
        return np.exp2(np.random.permutation(np.resize(levels, k // 32))).repeat(32)
    a = np.empty((k // 512, 16))
    for p in range(k // 512):
        a[p, :8] = np.random.permutation(np.resize(levels, 8))
        for g in range(8):
            far = levels[np.abs(levels - a[p, g]) >= 10]
            a[p, g + 8] = far[np.random.randint(len(far))]
    return np.exp2(a.ravel()).repeat(32)


def f64(x):
    return np.asarray(x).astype(np.float64)


def striped(idx):
    return np.tile(idx.reshape(-1, 16).T, (8, 1)).astype(np.uint16)


def unstriped(offs):
    return offs[:16].T.reshape(-1).astype(np.int64)


def pack_weight(w):
    k, n = w.shape
    w = f64(np.asarray(w, np.float32).astype(ml_dtypes.bfloat16)).reshape(k // 32, 32, n)
    amax = np.abs(w).max(1)
    byte = np.clip(np.where(amax > 0, np.frexp(amax)[1] - 1 + 127 - 7, 1), 1, 254)
    scaled = (w * np.exp2(127.0 - byte)[:, None, :]).reshape(k, n).astype(np.float32)
    words = np.ascontiguousarray(scaled.reshape(k // 512, 128, 4, n).transpose(0, 1, 3, 2)).astype(ml_dtypes.float8_e4m3fn).view(np.uint8)
    return words, np.ascontiguousarray(byte.astype(np.uint8).reshape(k // 512, 16, n))


def unpack_weight(words, scales):
    g, p, n, _ = words.shape
    vals = np.ascontiguousarray(words).view(ml_dtypes.float8_e4m3fn).astype(np.float64) * np.repeat(np.exp2(scales.astype(np.float64) - 127.0), 8, axis=1)[..., None]
    return vals.transpose(0, 1, 3, 2).reshape(g * 512, n)


def sigmoid(v):
    return 1.0 / (1.0 + np.exp(-np.maximum(v, -700.0)))

def planes(y):
    n, m = y.shape
    v = y.astype(np.float32).astype(ml_dtypes.bfloat16).astype(np.float64).reshape(n // 32, 32, m)
    top = np.abs(v).max(1)
    byte = np.clip(np.where(top > 0, np.frexp(top)[1] - 1 + 127 - 7, 1), 1, 254)
    codes = (v * np.exp2(127.0 - byte)[:, None, :]).reshape(n, m).astype(np.float32).astype(ml_dtypes.float8_e4m3fn).view(np.uint8)
    words = codes.reshape(n // 512, 128, 4, m).transpose(0, 1, 3, 2)
    return np.ascontiguousarray(words), np.ascontiguousarray(byte.astype(np.uint8).reshape(n // 512, 16, m))


K, T, S, N, H, W = 512, 2048, 512, 512, 512, 256


def setup_inputs():
    n = np.random.standard_normal
    s = mx_kscale(K)[:, None]
    u = mx_kscale(S)
    packed_xT = pack_weight(n((K, T)) * s)
    perm = np.random.permutation(N)
    return {
        "x_words": packed_xT[0],
        "x_scales": packed_xT[1],
        "wa": (n((K, H)) / np.sqrt(K) / s).astype(np.float32),
        "wb": (n((K, N)) / np.sqrt(K) / s).astype(np.float32),
        "gt": (np.random.uniform(0.5, 1.5, (S, 1)) * u[:, None]).astype(np.float32),
        "gi": (np.random.uniform(0.5, 1.5, (S, 1)) / u[:, None]).astype(np.float32),
        "sl": np.random.uniform(1.0, 2.0, (H, 1)).astype(np.float32),
        "th": (0.5 * n((H, 1))).astype(np.float32),
        "offs": striped(np.random.permutation(T)[:S]),
        "two": striped(np.random.permutation(T)[:S]),
        "n1": striped(np.random.permutation(H)),
        "n2": striped(np.random.permutation(H)),
        "n3": striped(perm[:W]),
        "n4": striped(perm[W:]),
    }


def reference(x_words, x_scales, wa, wb, gt, gi, sl, th, offs, two, n1, n2, n3, n4):
    xq = unpack_weight(x_words, x_scales)[:, unstriped(offs)]
    a = xq.T @ mxq(f64(wa), 0, "e4m3")
    pa = a[:, unstriped(n1)]
    pb = a[:, unstriped(n2)]
    z = f64(gt) * (np.maximum(np.minimum(a, pa), np.minimum(np.maximum(a, pa), pb)))
    x_two = unpack_weight(x_words, x_scales)[:, unstriped(two)]
    b = x_two.T @ mxq(f64(wb), 0, "e4m3")
    z2 = f64(gi) * b
    cv = 0.0625 * ((mxq(z, 0, "e4m3").T @ mxq(z2, 0, "e4m3")))
    pb2 = cv[:, unstriped(n4)]
    sg = sigmoid(f64(sl) * (cv[:, unstriped(n3)] - f64(th)))
    rb = pb2 - sg
    pa2 = cv[:, unstriped(n3)]
    sg2 = sigmoid(f64(sl) * (cv[:, unstriped(n4)] - f64(th)))
    ra = pa2 * sg2
    ds = np.zeros((H, N))
    ds[:, unstriped(n3)] = ra
    out = ds.copy()
    out[:, unstriped(n4)] = rb
    return (out,) + planes(out)

@@ -1,0 +1,243 @@
+from contextlib import ExitStack
+
+import concourse.mybir as mybir
+from concourse.masks import make_identity
+
+K, T, S, N, H, W = 512, 2048, 512, 512, 512, 256
+FLOPS = 2 * K * S * H + 2 * K * S * N + 2 * S * H * N
+
+F32 = mybir.dt.float32
+BF16 = mybir.dt.bfloat16
+I32 = mybir.dt.int32
+U32 = mybir.dt.uint32
+U16 = mybir.dt.uint16
+U8 = mybir.dt.uint8
+FP8X4 = mybir.dt.float8_e4m3fn_x4
+ALU = mybir.AluOpType
+ACT = mybir.ActivationFunctionType
+
+P = 128
+PACK = 4
+QUAD = 32
+HALF = 256
+CHUNKS = H // P
+LIST_ROWS = 16
+
+
+def tile_picked_mommedeod_none_po_kernel(
+    tc, x_words, x_scales, wa, wb, gt, gi, sl, th, offs, two, n1, n2, n3, n4, out_0, out_1, out_2
+):
+    nc = tc.nc
+    with ExitStack() as ctx:
+        keep = ctx.enter_context(tc.tile_pool(name="keep", bufs=1))
+        psum = ctx.enter_context(tc.psum_pool(name="psum", bufs=1))
+
+        def load_list(name, src):
+            tile = keep.tile(list(src.shape), U16, name=name)
+            nc.sync.dma_start(tile[:], src)
+            return tile
+
+        def load_weight_part(name, w, part, width):
+            raw = keep.tile([P, PACK, width], F32, name=name)
+            nc.sync.dma_start(out=raw[:], in_=w[:, part * width:(part + 1) * width].rearrange("(p j) c -> p j c", j=PACK))
+            return raw
+
+        table_scales = keep.tile([P, T], U8, name="table_scales", align_bytes=64)
+        nc.vector.memset(table_scales[:].bitcast(I32), 0)
+        staged_scales = keep.tile([P, T // 4], I32, name="staged_scales")
+        for q in range(4):
+            live = slice(QUAD * q, QUAD * q + 4)
+            nc.sync.dma_start(out=staged_scales[live, :], in_=x_scales[0][4 * q:4 * q + 4, :].bitcast(I32))
+            nc.vector.tensor_copy(out=table_scales[live, :].bitcast(I32), in_=staged_scales[live, :])
+        offs_t = load_list("offs_t", offs)
+        table_words = keep.tile([P, T], U32, name="table_words", align_bytes=64)
+        nc.sync.dma_start(out=table_words[:].bitcast(I32), in_=x_words[0].rearrange("p n r -> p (n r)").bitcast(I32))
+        wa_raw = [load_weight_part("wa_raw%d" % h, wa, h, P) for h in range(2)]
+        two_t = load_list("two_t", two)
+        wa_raw.extend([load_weight_part("wa_raw%d" % h, wa, h, P) for h in range(2, 4)])
+        wb_raw = [load_weight_part("wb_raw%d" % h, wb, h, HALF) for h in range(2)]
+        gt_t = keep.tile([P, PACK], F32, name="gt_t")
+        gi_t = keep.tile([P, PACK], F32, name="gi_t")
+        sl_t = keep.tile([P, CHUNKS], F32, name="sl_t")
+        th_t = keep.tile([P, CHUNKS], F32, name="th_t")
+        nc.gpsimd.dma_start(out=gt_t[:], in_=gt.rearrange("(p t) o -> p (t o)", t=PACK))
+        nc.gpsimd.dma_start(out=gi_t[:], in_=gi.rearrange("(p t) o -> p (t o)", t=PACK))
+        n1_t = load_list("n1_t", n1)
+        n2_t = load_list("n2_t", n2)
+        n3_t = load_list("n3_t", n3)
+        n4_t = load_list("n4_t", n4)
+        with nc.allow_non_contiguous_dma(reason="one value a row of cv"):
+            nc.sync.dma_start(out=sl_t[:], in_=sl.rearrange("(c m) o -> m (c o)", m=P))
+            nc.sync.dma_start(out=th_t[:], in_=th.rearrange("(c m) o -> m (c o)", m=P))
+        identity = keep.tile([P, P], F32, name="identity")
+        make_identity(nc, identity[:])
+
+        def pick_scales(name, entries):
+            tile = keep.tile([P, S], U8, name=name, align_bytes=64)
+            nc.vector.tensor_copy(tile[:].rearrange("p (t m) -> p m t", t=PACK), table_scales[:].indirect(entries[:]))
+            return tile
+
+        def pick_words(name, entries):
+            tile = keep.tile([P, S], U32, name=name, align_bytes=64)
+            nc.vector.tensor_copy(tile[:].rearrange("p (t m) -> p m t", t=PACK), table_words[:].indirect(entries[:]))
+            return tile
+
+        def round_weight(name, raw, on_scalar):
+            grouped = keep.tile([P, raw.shape[2], PACK], BF16, name=name, align_bytes=64)
+            dst = grouped[:].rearrange("p (c i) j -> p c j i", i=4)
+            src = raw[:].rearrange("p j (c i) -> p c j i", i=4)
+            if on_scalar:
+                nc.scalar.copy(out=dst, in_=src)
+            else:
+                nc.vector.tensor_copy(out=dst, in_=src)
+            return grouped
+
+        def quantize(codes, scales, grouped):
+            nc.vector.quantize_mx(out=codes.bitcast(FP8X4), scales=scales, in_=grouped.rearrange("p c j -> p (c j)"))
+
+        def product(out, lhs, lhs_scales, rhs, rhs_scales):
+            nc.tensor.matmul_mx(
+                out=out, lhsT=lhs.bitcast(FP8X4), lhsT_scale=lhs_scales, rhs=rhs.bitcast(FP8X4), rhs_scale=rhs_scales,
+                start=True, stop=True,
+            )
+
+        xa_scales = pick_scales("xa_scales", offs_t)
+        xa_words = pick_words("xa_words", offs_t)
+        wa_codes = keep.tile([P, H], U32, name="wa_codes", align_bytes=64)
+        wa_scales = keep.tile([P, H], U8, name="wa_scales", align_bytes=64)
+        wa_grouped = [round_weight("wa_grouped%d" % h, wa_raw[h], True) for h in range(4)]
+        for h in range(4):
+            cols = slice(h * P, (h + 1) * P)
+            quantize(wa_codes[:, cols], wa_scales[:, cols], wa_grouped[h][:])
+
+        xb_scales = pick_scales("xb_scales", two_t)
+        xb_words = pick_words("xb_words", two_t)
+        wb_codes = keep.tile([P, N], U32, name="wb_codes", align_bytes=64)
+        wb_scales = keep.tile([P, N], U8, name="wb_scales", align_bytes=64)
+        wb_grouped = [round_weight("wb_grouped%d" % h, wb_raw[h], h == 0) for h in range(2)]
+
+        ga = keep.tile([P, PACK, H], F32, name="ga")
+        acc_a = [psum.tile([P, H], F32, name="acc_a%d" % t) for t in range(PACK)]
+        for hb in range(H // P):
+            hcols = slice(hb * P, (hb + 1) * P)
+            for t in range(PACK):
+                cols = slice(t * P, (t + 1) * P)
+                product(acc_a[t][:, hcols], xa_words[:, cols], xa_scales[:, cols], wa_codes[:, hcols], wa_scales[:, hcols])
+        for t in range(PACK):
+            nc.scalar.activation(out=ga[:, t, :], in_=acc_a[t][:], func=ACT.Copy, scale=gt_t[:, t:t + 1])
+
+        z2_grouped = keep.tile([P, N, PACK], BF16, name="z2_grouped", align_bytes=64)
+        z2_codes = keep.tile([P, N], U32, name="z2_codes", align_bytes=64)
+        z2_scales = keep.tile([P, N], U8, name="z2_scales", align_bytes=64)
+        for h in range(2):
+            cols = slice(h * HALF, (h + 1) * HALF)
+            quantize(wb_codes[:, cols], wb_scales[:, cols], wb_grouped[h][:])
+        for nb in range(N // P):
+            ncols = slice(nb * P, (nb + 1) * P)
+            acc = psum.tile([P, PACK, P], F32, name="acc_b", tag="acc_b", bufs=2)
+            for t in range(PACK):
+                cols = slice(t * P, (t + 1) * P)
+                product(acc[:, t, :], xb_words[:, cols], xb_scales[:, cols], wb_codes[:, ncols], wb_scales[:, ncols])
+            nc.vector.tensor_tensor(
+                out=z2_grouped[:, ncols, :], in0=acc[:].rearrange("p t n -> p n t"),
+                in1=gi_t[:].unsqueeze(1).to_broadcast([P, P, PACK]), op=ALU.mult,
+            )
+        for h in range(2):
+            cols = slice(h * HALF, (h + 1) * HALF)
+            quantize(z2_codes[:, cols], z2_scales[:, cols], z2_grouped[:, cols, :])
+
+        bias_t = keep.tile([P, CHUNKS], F32, name="bias_t")
+        nc.vector.scalar_tensor_tensor(out=bias_t[:], in0=sl_t[:], scalar=-1.0, in1=th_t[:], op0=ALU.mult, op1=ALU.mult)
+
+        def make_z(c):
+            hcols = slice(c * P, (c + 1) * P)
+            lcols = slice(c * P // LIST_ROWS, (c + 1) * P // LIST_ROWS)
+            pa = keep.tile([P, PACK, P], F32, name="pa%d" % c, tag="pa", bufs=2)
+            pb = keep.tile([P, PACK, P], F32, name="pb%d" % c, tag="pb", bufs=2)
+            for t in range(PACK):
+                for dst, entries in ((pa, n1_t), (pb, n2_t)):
+                    src = ga[:, t, :].indirect(entries[:, lcols])
+                    if c < 2:
+                        nc.scalar.activation(out=dst[:, t, :], in_=src, func=ACT.Copy)
+                    else:
+                        nc.vector.tensor_copy(out=dst[:, t, :], in_=src)
+            ends = keep.tile([P, 2, PACK, P], F32, name="ends%d" % c, tag="zg%d" % (c - 1) if c else "ends", align_bytes=64)
+            lo, hi = ends[:, 0], ends[:, 1]
+            mid = keep.tile([P, PACK, P], F32, name="mid%d" % c)
+            z = keep.tile([P, PACK, P], BF16, name="z%d" % c)
+            nc.vector.tensor_tensor(out=hi, in0=pa[:], in1=pb[:], op=ALU.max)
+            nc.vector.tensor_tensor(out=lo, in0=pa[:], in1=pb[:], op=ALU.min)
+            nc.vector.tensor_tensor(out=mid[:], in0=hi, in1=ga[:, :, hcols], op=ALU.min)
+            nc.vector.tensor_tensor(out=z[:], in0=lo, in1=mid[:], op=ALU.max)
+            grouped = keep.tile([P, P, PACK], BF16, name="z_grouped%d" % c, tag="zg%d" % c, align_bytes=64)
+            nc.vector.tensor_copy(
+                out=grouped[:].rearrange("p (c i) j -> p c j i", i=4), in_=z[:].rearrange("p j (c i) -> p c j i", i=4)
+            )
+            codes = keep.tile([P, P], U32, name="z_codes%d" % c, align_bytes=64)
+            scales = keep.tile([P, P], U8, name="z_scales%d" % c, align_bytes=64)
+            quantize(codes[:], scales[:], grouped[:])
+            return codes, scales
+
+        def make_rows(c, z_codes, z_scales):
+            acc = psum.tile([P, N], F32, name="chain", tag="chain%d" % (c % 2))
+            product(acc[:], z_codes[:], z_scales[:], z2_codes[:], z2_scales[:])
+            cv = keep.tile([P, N], F32, name="cv%d" % c)
+            nc.vector.tensor_scalar(out=cv[:], in0=acc[:], scalar1=0.0625, scalar2=None, op0=ALU.mult)
+            slope, bias = sl_t[:, c:c + 1], bias_t[:, c:c + 1]
+            sg2 = keep.tile([P, W], F32, name="sg2_%d" % c)
+            pa2 = keep.tile([P, W], F32, name="pa2_%d" % c)
+            sg = keep.tile([P, W], F32, name="sg_%d" % c)
+            pb2 = keep.tile([P, W], F32, name="pb2_%d" % c)
+            ra = keep.tile([P, W], F32, name="ra%d" % c)
+            rb = keep.tile([P, W], F32, name="rb%d" % c)
+            nc.scalar.activation(out=sg2[:], in_=cv[:].indirect(n4_t[:]), func=ACT.Sigmoid, bias=bias, scale=slope)
+            nc.scalar.activation(out=pa2[:], in_=cv[:].indirect(n3_t[:]), func=ACT.Copy)
+            nc.gpsimd.tensor_tensor(out=ra[:], in0=pa2[:], in1=sg2[:], op=ALU.mult)
+            nc.scalar.activation(out=sg[:], in_=cv[:].indirect(n3_t[:]), func=ACT.Sigmoid, bias=bias, scale=slope)
+            nc.scalar.activation(out=pb2[:], in_=cv[:].indirect(n4_t[:]), func=ACT.Copy)
+            nc.gpsimd.tensor_tensor(out=rb[:], in0=pb2[:], in1=sg[:], op=ALU.subtract)
+            rows = keep.tile([P, N], F32, name="rows%d" % c)
+            nc.scalar.activation(out=rows[:].indirect(n3_t[:]), in_=ra[:], func=ACT.Copy)
+            nc.scalar.activation(out=rows[:].indirect(n4_t[:]), in_=rb[:], func=ACT.Copy)
+            nc.sync.dma_start(out=out_0[c * P:(c + 1) * P, :], in_=rows[:])
+            return rows
+
+        out_words = out_1[0].rearrange("l n r -> l (n r)").bitcast(I32)
+        out_scales = keep.tile([P, CHUNKS, P], U8, name="out_scales", align_bytes=64)
+
+        def make_planes(c, rows):
+            turned = psum.tile([P, N], F32, name="turned", tag="chain%d" % ((c + 1) % 2))
+            for nb in range(N // P):
+                cols = slice(nb * P, (nb + 1) * P)
+                nc.tensor.transpose(turned[:, cols], rows[:, cols], identity[:])
+            pairs = keep.tile([P, N], BF16, name="pairs%d" % c, tag="zg3" if c == 1 else "pairs%d" % c, align_bytes=64)
+            nc.vector.tensor_copy(
+                out=pairs[:].rearrange("p (u g e) -> p u g e", u=2, e=2),
+                in_=turned[:].rearrange("p (g u e) -> p u g e", u=2, e=2),
+            )
+            back = psum.tile([P, 2, P], F32, name="back", tag="acc_b", bufs=2)
+            for u in range(2):
+                nc.tensor.transpose(back[:, u, :], pairs[:].bitcast(F32)[:, u * P:(u + 1) * P], identity[:])
+            grouped = keep.tile([P, P * PACK], BF16, name="out_grouped%d" % c, align_bytes=64)
+            nc.vector.tensor_copy(
+                out=grouped[:].bitcast(F32).rearrange("p (n u) -> p n u", u=2), in_=back[:].rearrange("p u n -> p n u")
+            )
+            codes = keep.tile([P, P], U32, name="out_codes%d" % c, align_bytes=64)
+            nc.vector.quantize_mx(out=codes[:].bitcast(FP8X4), scales=out_scales[:, c, :], in_=grouped[:])
+            for nb in range(N // P):
+                nc.sync.dma_start(
+                    out=out_words[QUAD * c:QUAD * (c + 1), nb * P:(nb + 1) * P],
+                    in_=codes[QUAD * nb:QUAD * (nb + 1), :].bitcast(I32),
+                )
+
+        rows = []
+        for c in range(CHUNKS):
+            z_codes, z_scales = make_z(c)
+            rows.append(make_rows(c, z_codes, z_scales))
+        for c in range(CHUNKS):
+            make_planes(c, rows[c])
+        for nb in range(N // P):
+            nc.scalar.dma_start(
+                out=out_2[0][:, nb * P:(nb + 1) * P].bitcast(I32).rearrange("(c r) w -> r c w", r=4),
+                in_=out_scales[QUAD * nb:QUAD * nb + 4, :, :].bitcast(I32),
+            )

@@ -72,18 +72,18 @@ def tile_picked_mommedeod_none_po_kernel(
         identity = keep.tile([P, P], F32, name="identity")
         make_identity(nc, identity[:])
 
-        def pick_scales(name, entries):
-            tile = keep.tile([P, S], U8, name=name, align_bytes=64)
+        def pick_scales(name, entries, tag):
+            tile = keep.tile([P, S], U8, name=name, tag=tag, align_bytes=64)
             nc.vector.tensor_copy(tile[:].rearrange("p (t m) -> p m t", t=PACK), table_scales[:].indirect(entries[:]))
             return tile
 
-        def pick_words(name, entries):
-            tile = keep.tile([P, S], U32, name=name, align_bytes=64)
+        def pick_words(name, entries, tag):
+            tile = keep.tile([P, S], U32, name=name, tag=tag, align_bytes=64)
             nc.vector.tensor_copy(tile[:].rearrange("p (t m) -> p m t", t=PACK), table_words[:].indirect(entries[:]))
             return tile
 
         def round_weight(name, raw, on_scalar):
-            grouped = keep.tile([P, raw.shape[2], PACK], BF16, name=name, align_bytes=64)
+            grouped = keep.tile([P, raw.shape[2], PACK], BF16, name=name, tag=name, align_bytes=64)
             dst = grouped[:].rearrange("p (c i) j -> p c j i", i=4)
             src = raw[:].rearrange("p j (c i) -> p c j i", i=4)
             if on_scalar:
@@ -101,17 +101,17 @@ def tile_picked_mommedeod_none_po_kernel(
                 start=True, stop=True,
             )
 
-        xa_scales = pick_scales("xa_scales", offs_t)
-        xa_words = pick_words("xa_words", offs_t)
-        wa_codes = keep.tile([P, H], U32, name="wa_codes", align_bytes=64)
-        wa_scales = keep.tile([P, H], U8, name="wa_scales", align_bytes=64)
+        xa_scales = pick_scales("xa_scales", offs_t, "xa_scales")
+        xa_words = pick_words("xa_words", offs_t, "xa_words")
+        wa_codes = keep.tile([P, H], U32, name="wa_codes", tag="wa_codes", align_bytes=64)
+        wa_scales = keep.tile([P, H], U8, name="wa_scales", tag="wa_scales", align_bytes=64)
         wa_grouped = [round_weight("wa_grouped%d" % h, wa_raw[h], True) for h in range(4)]
         for h in range(4):
             cols = slice(h * P, (h + 1) * P)
             quantize(wa_codes[:, cols], wa_scales[:, cols], wa_grouped[h][:])
 
-        xb_scales = pick_scales("xb_scales", two_t)
-        xb_words = pick_words("xb_words", two_t)
+        xb_scales = pick_scales("xb_scales", two_t, "wa_grouped0")
+        xb_words = pick_words("xb_words", two_t, "wa_grouped3")
         wb_codes = keep.tile([P, N], U32, name="wb_codes", align_bytes=64)
         wb_scales = keep.tile([P, N], U8, name="wb_scales", align_bytes=64)
         wb_grouped = [round_weight("wb_grouped%d" % h, wb_raw[h], h == 0) for h in range(2)]
@@ -152,29 +152,29 @@ def tile_picked_mommedeod_none_po_kernel(
         def make_z(c):
             hcols = slice(c * P, (c + 1) * P)
             lcols = slice(c * P // LIST_ROWS, (c + 1) * P // LIST_ROWS)
-            pa = keep.tile([P, PACK, P], F32, name="pa%d" % c, tag="pa", bufs=2)
-            pb = keep.tile([P, PACK, P], F32, name="pb%d" % c, tag="pb", bufs=2)
+            pa = keep.tile([P, PACK, P], F32, name="pa%d" % c, tag=("pa0", "xa_words", "wa_codes", "z_codes1")[c], align_bytes=64)
+            pb = keep.tile([P, PACK, P], F32, name="pb%d" % c, tag=("pb0", "xa_scales", "z_codes0", "z_codes2")[c], align_bytes=64)
             for t in range(PACK):
                 for dst, entries in ((pa, n1_t), (pb, n2_t)):
                     src = ga[:, t, :].indirect(entries[:, lcols])
-                    if c < 2:
+                    if c < 2 or (c == 2 and dst is pa):
                         nc.scalar.activation(out=dst[:, t, :], in_=src, func=ACT.Copy)
                     else:
                         nc.vector.tensor_copy(out=dst[:, t, :], in_=src)
-            ends = keep.tile([P, 2, PACK, P], F32, name="ends%d" % c, tag="zg%d" % (c - 1) if c else "ends", align_bytes=64)
-            lo, hi = ends[:, 0], ends[:, 1]
+            lo = keep.tile([P, PACK, P], F32, name="lo%d" % c, tag="z_scales%d" % (c - 1) if c else "lo0", align_bytes=64)
+            hi = keep.tile([P, PACK, P], F32, name="hi%d" % c, tag="zg%d" % (c - 1) if c else "hi0", align_bytes=64)
             mid = keep.tile([P, PACK, P], F32, name="mid%d" % c)
             z = keep.tile([P, PACK, P], BF16, name="z%d" % c)
-            nc.vector.tensor_tensor(out=hi, in0=pa[:], in1=pb[:], op=ALU.max)
-            nc.vector.tensor_tensor(out=lo, in0=pa[:], in1=pb[:], op=ALU.min)
-            nc.vector.tensor_tensor(out=mid[:], in0=hi, in1=ga[:, :, hcols], op=ALU.min)
-            nc.vector.tensor_tensor(out=z[:], in0=lo, in1=mid[:], op=ALU.max)
+            nc.vector.tensor_tensor(out=hi[:], in0=pa[:], in1=pb[:], op=ALU.max)
+            nc.vector.tensor_tensor(out=lo[:], in0=pa[:], in1=pb[:], op=ALU.min)
+            nc.vector.tensor_tensor(out=mid[:], in0=hi[:], in1=ga[:, :, hcols], op=ALU.min)
+            nc.vector.tensor_tensor(out=z[:], in0=lo[:], in1=mid[:], op=ALU.max)
             grouped = keep.tile([P, P, PACK], BF16, name="z_grouped%d" % c, tag="zg%d" % c, align_bytes=64)
             nc.vector.tensor_copy(
                 out=grouped[:].rearrange("p (c i) j -> p c j i", i=4), in_=z[:].rearrange("p j (c i) -> p c j i", i=4)
             )
-            codes = keep.tile([P, P], U32, name="z_codes%d" % c, align_bytes=64)
-            scales = keep.tile([P, P], U8, name="z_scales%d" % c, align_bytes=64)
+            codes = keep.tile([P, P], U32, name="z_codes%d" % c, tag="z_codes%d" % c, align_bytes=64)
+            scales = keep.tile([P, P], U8, name="z_scales%d" % c, tag="z_scales%d" % c, align_bytes=64)
             quantize(codes[:], scales[:], grouped[:])
             return codes, scales
 

@@ -55,15 +55,15 @@ def tile_picked_mommedeod_none_po_kernel(
         wa_raw = [load_weight_part("wa_raw%d" % h, wa, h, P) for h in range(2)]
         two_t = load_list("two_t", two)
         wa_raw.extend([load_weight_part("wa_raw%d" % h, wa, h, P) for h in range(2, 4)])
-        wb_raw = [load_weight_part("wb_raw%d" % h, wb, h, HALF) for h in range(2)]
         gt_t = keep.tile([P, PACK], F32, name="gt_t")
         gi_t = keep.tile([P, PACK], F32, name="gi_t")
         sl_t = keep.tile([P, CHUNKS], F32, name="sl_t")
         th_t = keep.tile([P, CHUNKS], F32, name="th_t")
-        nc.gpsimd.dma_start(out=gt_t[:], in_=gt.rearrange("(p t) o -> p (t o)", t=PACK))
-        nc.gpsimd.dma_start(out=gi_t[:], in_=gi.rearrange("(p t) o -> p (t o)", t=PACK))
+        nc.sync.dma_start(out=gt_t[:], in_=gt.rearrange("(p t) o -> p (t o)", t=PACK))
         n1_t = load_list("n1_t", n1)
+        wb_raw = [load_weight_part("wb_raw%d" % h, wb, h, HALF) for h in range(2)]
         n2_t = load_list("n2_t", n2)
+        nc.sync.dma_start(out=gi_t[:], in_=gi.rearrange("(p t) o -> p (t o)", t=PACK))
         n3_t = load_list("n3_t", n3)
         n4_t = load_list("n4_t", n4)
         with nc.allow_non_contiguous_dma(reason="one value a row of cv"):
@@ -149,53 +149,66 @@ def tile_picked_mommedeod_none_po_kernel(
         bias_t = keep.tile([P, CHUNKS], F32, name="bias_t")
         nc.vector.scalar_tensor_tensor(out=bias_t[:], in0=sl_t[:], scalar=-1.0, in1=th_t[:], op0=ALU.mult, op1=ALU.mult)
 
-        def make_z(c):
-            hcols = slice(c * P, (c + 1) * P)
+        pa_tags = ("pa0", "xa_words", "wa_codes", "z_scales0")
+        pb_tags = ("pb0", "xa_scales", "wa_scales", "z_scales1")
+
+        def median_ends(c):
             lcols = slice(c * P // LIST_ROWS, (c + 1) * P // LIST_ROWS)
-            pa = keep.tile([P, PACK, P], F32, name="pa%d" % c, tag=("pa0", "xa_words", "wa_codes", "z_codes1")[c], align_bytes=64)
-            pb = keep.tile([P, PACK, P], F32, name="pb%d" % c, tag=("pb0", "xa_scales", "z_codes0", "z_codes2")[c], align_bytes=64)
+            pa = keep.tile([P, PACK, P], F32, name="pa%d" % c, tag=pa_tags[c], align_bytes=64)
+            pb = keep.tile([P, PACK, P], F32, name="pb%d" % c, tag=pb_tags[c], align_bytes=64)
             for t in range(PACK):
                 for dst, entries in ((pa, n1_t), (pb, n2_t)):
                     src = ga[:, t, :].indirect(entries[:, lcols])
-                    if c < 2 or (c == 2 and dst is pa):
+                    if c < CHUNKS - 1:
                         nc.scalar.activation(out=dst[:, t, :], in_=src, func=ACT.Copy)
                     else:
                         nc.vector.tensor_copy(out=dst[:, t, :], in_=src)
             lo = keep.tile([P, PACK, P], F32, name="lo%d" % c, tag="z_scales%d" % (c - 1) if c else "lo0", align_bytes=64)
             hi = keep.tile([P, PACK, P], F32, name="hi%d" % c, tag="zg%d" % (c - 1) if c else "hi0", align_bytes=64)
-            mid = keep.tile([P, PACK, P], F32, name="mid%d" % c)
-            z = keep.tile([P, PACK, P], BF16, name="z%d" % c)
             nc.vector.tensor_tensor(out=hi[:], in0=pa[:], in1=pb[:], op=ALU.max)
             nc.vector.tensor_tensor(out=lo[:], in0=pa[:], in1=pb[:], op=ALU.min)
-            nc.vector.tensor_tensor(out=mid[:], in0=hi[:], in1=ga[:, :, hcols], op=ALU.min)
-            nc.vector.tensor_tensor(out=z[:], in0=lo[:], in1=mid[:], op=ALU.max)
+            return lo, hi
+
+        def median(c, lo, hi):
+            mid = keep.tile([P, PACK, P], F32, name="mid%d" % c, tag="mid%d" % c, align_bytes=64)
+            nc.vector.tensor_tensor(out=mid[:], in0=hi[:], in1=ga[:, :, c * P:(c + 1) * P], op=ALU.min)
             grouped = keep.tile([P, P, PACK], BF16, name="z_grouped%d" % c, tag="zg%d" % c, align_bytes=64)
-            nc.vector.tensor_copy(
-                out=grouped[:].rearrange("p (c i) j -> p c j i", i=4), in_=z[:].rearrange("p j (c i) -> p c j i", i=4)
+            nc.vector.tensor_tensor(
+                out=grouped[:].rearrange("p (c i) j -> p c j i", i=4),
+                in0=lo[:].rearrange("p j (c i) -> p c j i", i=4),
+                in1=mid[:].rearrange("p j (c i) -> p c j i", i=4),
+                op=ALU.max,
             )
+            return grouped
+
+        def make_cv(c, grouped):
             codes = keep.tile([P, P], U32, name="z_codes%d" % c, tag="z_codes%d" % c, align_bytes=64)
             scales = keep.tile([P, P], U8, name="z_scales%d" % c, tag="z_scales%d" % c, align_bytes=64)
             quantize(codes[:], scales[:], grouped[:])
-            return codes, scales
-
-        def make_rows(c, z_codes, z_scales):
             acc = psum.tile([P, N], F32, name="chain", tag="chain%d" % (c % 2))
-            product(acc[:], z_codes[:], z_scales[:], z2_codes[:], z2_scales[:])
+            product(acc[:], codes[:], scales[:], z2_codes[:], z2_scales[:])
             cv = keep.tile([P, N], F32, name="cv%d" % c)
             nc.vector.tensor_scalar(out=cv[:], in0=acc[:], scalar1=0.0625, scalar2=None, op0=ALU.mult)
+            return cv
+
+        def fetch(c, cv):
             slope, bias = sl_t[:, c:c + 1], bias_t[:, c:c + 1]
             sg2 = keep.tile([P, W], F32, name="sg2_%d" % c)
             pa2 = keep.tile([P, W], F32, name="pa2_%d" % c)
             sg = keep.tile([P, W], F32, name="sg_%d" % c)
             pb2 = keep.tile([P, W], F32, name="pb2_%d" % c)
-            ra = keep.tile([P, W], F32, name="ra%d" % c)
-            rb = keep.tile([P, W], F32, name="rb%d" % c)
             nc.scalar.activation(out=sg2[:], in_=cv[:].indirect(n4_t[:]), func=ACT.Sigmoid, bias=bias, scale=slope)
             nc.scalar.activation(out=pa2[:], in_=cv[:].indirect(n3_t[:]), func=ACT.Copy)
-            nc.gpsimd.tensor_tensor(out=ra[:], in0=pa2[:], in1=sg2[:], op=ALU.mult)
             nc.scalar.activation(out=sg[:], in_=cv[:].indirect(n3_t[:]), func=ACT.Sigmoid, bias=bias, scale=slope)
             nc.scalar.activation(out=pb2[:], in_=cv[:].indirect(n4_t[:]), func=ACT.Copy)
-            nc.gpsimd.tensor_tensor(out=rb[:], in0=pb2[:], in1=sg[:], op=ALU.subtract)
+            return sg2, pa2, sg, pb2
+
+        def combine(name, tag, left, right, op):
+            tile = keep.tile([P, W], F32, name=name, tag=tag, align_bytes=64)
+            nc.vector.tensor_tensor(out=tile[:], in0=left[:], in1=right[:], op=op)
+            return tile
+
+        def put_back(c, ra, rb):
             rows = keep.tile([P, N], F32, name="rows%d" % c)
             nc.scalar.activation(out=rows[:].indirect(n3_t[:]), in_=ra[:], func=ACT.Copy)
             nc.scalar.activation(out=rows[:].indirect(n4_t[:]), in_=rb[:], func=ACT.Copy)
@@ -231,9 +244,19 @@ def tile_picked_mommedeod_none_po_kernel(
                 )
 
         rows = []
+        cv = make_cv(0, median(0, *median_ends(0)))
         for c in range(CHUNKS):
-            z_codes, z_scales = make_z(c)
-            rows.append(make_rows(c, z_codes, z_scales))
+            last = c == CHUNKS - 1
+            sg2, pa2, sg, pb2 = fetch(c, cv)
+            if not last:
+                lo, hi = median_ends(c + 1)
+            ra = combine("ra%d" % c, "ra_last" if last else pa_tags[c + 1], pa2, sg2, ALU.mult)
+            if not last:
+                grouped = median(c + 1, lo, hi)
+            rb = combine("rb%d" % c, "rb_last" if last else "mid%d" % (c + 1), pb2, sg, ALU.subtract)
+            rows.append(put_back(c, ra, rb))
+            if not last:
+                cv = make_cv(c + 1, grouped)
         for c in range(CHUNKS):
             make_planes(c, rows[c])
         for nb in range(N // P):

@@ -60,8 +60,8 @@ def tile_picked_mommedeod_none_po_kernel(
         sl_t = keep.tile([P, CHUNKS], F32, name="sl_t")
         th_t = keep.tile([P, CHUNKS], F32, name="th_t")
         nc.sync.dma_start(out=gt_t[:], in_=gt.rearrange("(p t) o -> p (t o)", t=PACK))
-        n1_t = load_list("n1_t", n1)
         wb_raw = [load_weight_part("wb_raw%d" % h, wb, h, HALF) for h in range(2)]
+        n1_t = load_list("n1_t", n1)
         n2_t = load_list("n2_t", n2)
         nc.sync.dma_start(out=gi_t[:], in_=gi.rearrange("(p t) o -> p (t o)", t=PACK))
         n3_t = load_list("n3_t", n3)
@@ -114,7 +114,6 @@ def tile_picked_mommedeod_none_po_kernel(
         xb_words = pick_words("xb_words", two_t, "wa_grouped3")
         wb_codes = keep.tile([P, N], U32, name="wb_codes", align_bytes=64)
         wb_scales = keep.tile([P, N], U8, name="wb_scales", align_bytes=64)
-        wb_grouped = [round_weight("wb_grouped%d" % h, wb_raw[h], h == 0) for h in range(2)]
 
         ga = keep.tile([P, PACK, H], F32, name="ga")
         acc_a = [psum.tile([P, H], F32, name="acc_a%d" % t) for t in range(PACK)]
@@ -130,48 +129,44 @@ def tile_picked_mommedeod_none_po_kernel(
         z2_codes = keep.tile([P, N], U32, name="z2_codes", align_bytes=64)
         z2_scales = keep.tile([P, N], U8, name="z2_scales", align_bytes=64)
         for h in range(2):
-            cols = slice(h * HALF, (h + 1) * HALF)
-            quantize(wb_codes[:, cols], wb_scales[:, cols], wb_grouped[h][:])
-        for nb in range(N // P):
-            ncols = slice(nb * P, (nb + 1) * P)
-            acc = psum.tile([P, PACK, P], F32, name="acc_b", tag="acc_b", bufs=2)
-            for t in range(PACK):
-                cols = slice(t * P, (t + 1) * P)
-                product(acc[:, t, :], xb_words[:, cols], xb_scales[:, cols], wb_codes[:, ncols], wb_scales[:, ncols])
-            nc.vector.tensor_tensor(
-                out=z2_grouped[:, ncols, :], in0=acc[:].rearrange("p t n -> p n t"),
-                in1=gi_t[:].unsqueeze(1).to_broadcast([P, P, PACK]), op=ALU.mult,
-            )
-        for h in range(2):
-            cols = slice(h * HALF, (h + 1) * HALF)
-            quantize(z2_codes[:, cols], z2_scales[:, cols], z2_grouped[:, cols, :])
+            half = slice(h * HALF, (h + 1) * HALF)
+            quantize(wb_codes[:, half], wb_scales[:, half], round_weight("wb_grouped%d" % h, wb_raw[h], False)[:])
+            for nb in (2 * h, 2 * h + 1):
+                ncols = slice(nb * P, (nb + 1) * P)
+                acc = psum.tile([P, PACK, P], F32, name="acc_b", tag="acc_b", bufs=2)
+                for t in range(PACK):
+                    cols = slice(t * P, (t + 1) * P)
+                    product(acc[:, t, :], xb_words[:, cols], xb_scales[:, cols], wb_codes[:, ncols], wb_scales[:, ncols])
+                nc.vector.tensor_tensor(
+                    out=z2_grouped[:, ncols, :], in0=acc[:].rearrange("p t n -> p n t"),
+                    in1=gi_t[:].unsqueeze(1).to_broadcast([P, P, PACK]), op=ALU.mult,
+                )
+            quantize(z2_codes[:, half], z2_scales[:, half], z2_grouped[:, half, :])
 
         bias_t = keep.tile([P, CHUNKS], F32, name="bias_t")
         nc.vector.scalar_tensor_tensor(out=bias_t[:], in0=sl_t[:], scalar=-1.0, in1=th_t[:], op0=ALU.mult, op1=ALU.mult)
 
-        pa_tags = ("pa0", "xa_words", "wa_codes", "z_scales0")
-        pb_tags = ("pb0", "xa_scales", "wa_scales", "z_scales1")
-
-        def median_ends(c):
-            lcols = slice(c * P // LIST_ROWS, (c + 1) * P // LIST_ROWS)
-            pa = keep.tile([P, PACK, P], F32, name="pa%d" % c, tag=pa_tags[c], align_bytes=64)
-            pb = keep.tile([P, PACK, P], F32, name="pb%d" % c, tag=pb_tags[c], align_bytes=64)
+        def look_up(name, tag, entries, first, count, on_scalar):
+            picked = keep.tile([P, PACK, count * P], F32, name=name, tag=tag, align_bytes=64)
+            lcols = slice(first * P // LIST_ROWS, (first + count) * P // LIST_ROWS)
             for t in range(PACK):
-                for dst, entries in ((pa, n1_t), (pb, n2_t)):
-                    src = ga[:, t, :].indirect(entries[:, lcols])
-                    if c < CHUNKS - 1:
-                        nc.scalar.activation(out=dst[:, t, :], in_=src, func=ACT.Copy)
-                    else:
-                        nc.vector.tensor_copy(out=dst[:, t, :], in_=src)
+                src = ga[:, t, :].indirect(entries[:, lcols])
+                if on_scalar:
+                    nc.scalar.activation(out=picked[:, t, :], in_=src, func=ACT.Copy)
+                else:
+                    nc.vector.tensor_copy(out=picked[:, t, :], in_=src)
+            return [picked[:, :, i * P:(i + 1) * P] for i in range(count)]
+
+        def clamp(c, pa, pb):
             lo = keep.tile([P, PACK, P], F32, name="lo%d" % c, tag="z_scales%d" % (c - 1) if c else "lo0", align_bytes=64)
             hi = keep.tile([P, PACK, P], F32, name="hi%d" % c, tag="zg%d" % (c - 1) if c else "hi0", align_bytes=64)
-            nc.vector.tensor_tensor(out=hi[:], in0=pa[:], in1=pb[:], op=ALU.max)
-            nc.vector.tensor_tensor(out=lo[:], in0=pa[:], in1=pb[:], op=ALU.min)
-            return lo, hi
-
-        def median(c, lo, hi):
             mid = keep.tile([P, PACK, P], F32, name="mid%d" % c, tag="mid%d" % c, align_bytes=64)
+            nc.vector.tensor_tensor(out=hi[:], in0=pa, in1=pb, op=ALU.max)
+            nc.vector.tensor_tensor(out=lo[:], in0=pa, in1=pb, op=ALU.min)
             nc.vector.tensor_tensor(out=mid[:], in0=hi[:], in1=ga[:, :, c * P:(c + 1) * P], op=ALU.min)
+            return lo, mid
+
+        def median(c, lo, mid):
             grouped = keep.tile([P, P, PACK], BF16, name="z_grouped%d" % c, tag="zg%d" % c, align_bytes=64)
             nc.vector.tensor_tensor(
                 out=grouped[:].rearrange("p (c i) j -> p c j i", i=4),
@@ -243,16 +238,23 @@ def tile_picked_mommedeod_none_po_kernel(
                     in_=codes[QUAD * nb:QUAD * (nb + 1), :].bitcast(I32),
                 )
 
+        pa = look_up("pa0", "pa0", n1_t, 0, 1, True)
+        pb = look_up("pb0", "pb0", n2_t, 0, 1, True)
+        cv = make_cv(0, median(0, *clamp(0, pa[0], pb[0])))
+        pa.extend(look_up("pa12", "xa_words", n1_t, 1, 2, True))
+        pb.extend(look_up("pb12", "xa_scales", n2_t, 1, 2, True))
         rows = []
-        cv = make_cv(0, median(0, *median_ends(0)))
         for c in range(CHUNKS):
             last = c == CHUNKS - 1
             sg2, pa2, sg, pb2 = fetch(c, cv)
+            if c == CHUNKS - 2:
+                pa.extend(look_up("pa3", "z_scales0", n1_t, 3, 1, False))
+                pb.extend(look_up("pb3", "z_scales1", n2_t, 3, 1, False))
             if not last:
-                lo, hi = median_ends(c + 1)
-            ra = combine("ra%d" % c, "ra_last" if last else pa_tags[c + 1], pa2, sg2, ALU.mult)
+                lo, mid = clamp(c + 1, pa[c + 1], pb[c + 1])
+            ra = combine("ra%d" % c, "ra_last" if last else "zg%d" % c, pa2, sg2, ALU.mult)
             if not last:
-                grouped = median(c + 1, lo, hi)
+                grouped = median(c + 1, lo, mid)
             rb = combine("rb%d" % c, "rb_last" if last else "mid%d" % (c + 1), pb2, sg, ALU.subtract)
             rows.append(put_back(c, ra, rb))
             if not last:

from contextlib import ExitStack

import concourse.mybir as mybir
from concourse.masks import make_identity

K, T, S, N, H, W = 512, 2048, 512, 512, 512, 256
FLOPS = 2 * K * S * H + 2 * K * S * N + 2 * S * H * N

F32 = mybir.dt.float32
BF16 = mybir.dt.bfloat16
I32 = mybir.dt.int32
U32 = mybir.dt.uint32
U16 = mybir.dt.uint16
U8 = mybir.dt.uint8
FP8X4 = mybir.dt.float8_e4m3fn_x4
ALU = mybir.AluOpType
ACT = mybir.ActivationFunctionType

P = 128
PACK = 4
QUAD = 32
HALF = 256
CHUNKS = H // P
LIST_ROWS = 16


def tile_picked_mommedeod_none_po_kernel(
    tc, x_words, x_scales, wa, wb, gt, gi, sl, th, offs, two, n1, n2, n3, n4, out_0, out_1, out_2
):
    nc = tc.nc
    with ExitStack() as ctx:
        keep = ctx.enter_context(tc.tile_pool(name="keep", bufs=1))
        psum = ctx.enter_context(tc.psum_pool(name="psum", bufs=1))

        def load_list(name, src):
            tile = keep.tile(list(src.shape), U16, name=name)
            nc.sync.dma_start(tile[:], src)
            return tile

        def load_weight_part(name, w, part, width):
            raw = keep.tile([P, PACK, width], F32, name=name)
            nc.sync.dma_start(out=raw[:], in_=w[:, part * width:(part + 1) * width].rearrange("(p j) c -> p j c", j=PACK))
            return raw

        table_scales = keep.tile([P, T], U8, name="table_scales", align_bytes=64)
        nc.vector.memset(table_scales[:].bitcast(I32), 0)
        staged_scales = keep.tile([P, T // 4], I32, name="staged_scales")
        for q in range(4):
            live = slice(QUAD * q, QUAD * q + 4)
            nc.sync.dma_start(out=staged_scales[live, :], in_=x_scales[0][4 * q:4 * q + 4, :].bitcast(I32))
            nc.vector.tensor_copy(out=table_scales[live, :].bitcast(I32), in_=staged_scales[live, :])
        offs_t = load_list("offs_t", offs)
        table_words = keep.tile([P, T], U32, name="table_words", align_bytes=64)
        nc.sync.dma_start(out=table_words[:].bitcast(I32), in_=x_words[0].rearrange("p n r -> p (n r)").bitcast(I32))
        wa_raw = [load_weight_part("wa_raw%d" % h, wa, h, P) for h in range(2)]
        two_t = load_list("two_t", two)
        wa_raw.extend([load_weight_part("wa_raw%d" % h, wa, h, P) for h in range(2, 4)])
        gt_t = keep.tile([P, PACK], F32, name="gt_t")
        gi_t = keep.tile([P, PACK], F32, name="gi_t")
        sl_t = keep.tile([P, CHUNKS], F32, name="sl_t")
        th_t = keep.tile([P, CHUNKS], F32, name="th_t")
        nc.sync.dma_start(out=gt_t[:], in_=gt.rearrange("(p t) o -> p (t o)", t=PACK))
        wb_raw = [load_weight_part("wb_raw%d" % h, wb, h, HALF) for h in range(2)]
        n1_t = load_list("n1_t", n1)
        n2_t = load_list("n2_t", n2)
        nc.sync.dma_start(out=gi_t[:], in_=gi.rearrange("(p t) o -> p (t o)", t=PACK))
        n3_t = load_list("n3_t", n3)
        n4_t = load_list("n4_t", n4)
        with nc.allow_non_contiguous_dma(reason="one value a row of cv"):
            nc.sync.dma_start(out=sl_t[:], in_=sl.rearrange("(c m) o -> m (c o)", m=P))
            nc.sync.dma_start(out=th_t[:], in_=th.rearrange("(c m) o -> m (c o)", m=P))
        identity = keep.tile([P, P], F32, name="identity")
        make_identity(nc, identity[:])

        def pick_scales(name, entries, tag):
            tile = keep.tile([P, S], U8, name=name, tag=tag, align_bytes=64)
            nc.vector.tensor_copy(tile[:].rearrange("p (t m) -> p m t", t=PACK), table_scales[:].indirect(entries[:]))
            return tile

        def pick_words(name, entries, tag):
            tile = keep.tile([P, S], U32, name=name, tag=tag, align_bytes=64)
            nc.vector.tensor_copy(tile[:].rearrange("p (t m) -> p m t", t=PACK), table_words[:].indirect(entries[:]))
            return tile

        def round_weight(name, raw, on_scalar):
            grouped = keep.tile([P, raw.shape[2], PACK], BF16, name=name, tag=name, align_bytes=64)
            dst = grouped[:].rearrange("p (c i) j -> p c j i", i=4)
            src = raw[:].rearrange("p j (c i) -> p c j i", i=4)
            if on_scalar:
                nc.scalar.copy(out=dst, in_=src)
            else:
                nc.vector.tensor_copy(out=dst, in_=src)
            return grouped

        def quantize(codes, scales, grouped):
            nc.vector.quantize_mx(out=codes.bitcast(FP8X4), scales=scales, in_=grouped.rearrange("p c j -> p (c j)"))

        def product(out, lhs, lhs_scales, rhs, rhs_scales):
            nc.tensor.matmul_mx(
                out=out, lhsT=lhs.bitcast(FP8X4), lhsT_scale=lhs_scales, rhs=rhs.bitcast(FP8X4), rhs_scale=rhs_scales,
                start=True, stop=True,
            )

        xa_scales = pick_scales("xa_scales", offs_t, "xa_scales")
        xa_words = pick_words("xa_words", offs_t, "xa_words")
        wa_codes = keep.tile([P, H], U32, name="wa_codes", tag="wa_codes", align_bytes=64)
        wa_scales = keep.tile([P, H], U8, name="wa_scales", tag="wa_scales", align_bytes=64)
        wa_grouped = [round_weight("wa_grouped%d" % h, wa_raw[h], True) for h in range(4)]
        for h in range(4):
            cols = slice(h * P, (h + 1) * P)
            quantize(wa_codes[:, cols], wa_scales[:, cols], wa_grouped[h][:])

        xb_scales = pick_scales("xb_scales", two_t, "wa_grouped0")
        xb_words = pick_words("xb_words", two_t, "wa_grouped3")
        wb_codes = keep.tile([P, N], U32, name="wb_codes", align_bytes=64)
        wb_scales = keep.tile([P, N], U8, name="wb_scales", align_bytes=64)

        ga = keep.tile([P, PACK, H], F32, name="ga")
        acc_a = [psum.tile([P, H], F32, name="acc_a%d" % t) for t in range(PACK)]
        for hb in range(H // P):
            hcols = slice(hb * P, (hb + 1) * P)
            for t in range(PACK):
                cols = slice(t * P, (t + 1) * P)
                product(acc_a[t][:, hcols], xa_words[:, cols], xa_scales[:, cols], wa_codes[:, hcols], wa_scales[:, hcols])
        for t in range(PACK):
            nc.scalar.activation(out=ga[:, t, :], in_=acc_a[t][:], func=ACT.Copy, scale=gt_t[:, t:t + 1])

        z2_grouped = keep.tile([P, N, PACK], BF16, name="z2_grouped", align_bytes=64)
        z2_codes = keep.tile([P, N], U32, name="z2_codes", align_bytes=64)
        z2_scales = keep.tile([P, N], U8, name="z2_scales", align_bytes=64)
        for h in range(2):
            half = slice(h * HALF, (h + 1) * HALF)
            quantize(wb_codes[:, half], wb_scales[:, half], round_weight("wb_grouped%d" % h, wb_raw[h], False)[:])
            for nb in (2 * h, 2 * h + 1):
                ncols = slice(nb * P, (nb + 1) * P)
                acc = psum.tile([P, PACK, P], F32, name="acc_b", tag="acc_b", bufs=2)
                for t in range(PACK):
                    cols = slice(t * P, (t + 1) * P)
                    product(acc[:, t, :], xb_words[:, cols], xb_scales[:, cols], wb_codes[:, ncols], wb_scales[:, ncols])
                nc.vector.tensor_tensor(
                    out=z2_grouped[:, ncols, :], in0=acc[:].rearrange("p t n -> p n t"),
                    in1=gi_t[:].unsqueeze(1).to_broadcast([P, P, PACK]), op=ALU.mult,
                )
            quantize(z2_codes[:, half], z2_scales[:, half], z2_grouped[:, half, :])

        bias_t = keep.tile([P, CHUNKS], F32, name="bias_t")
        nc.vector.scalar_tensor_tensor(out=bias_t[:], in0=sl_t[:], scalar=-1.0, in1=th_t[:], op0=ALU.mult, op1=ALU.mult)

        def look_up(name, tag, entries, first, count, on_scalar):
            picked = keep.tile([P, PACK, count * P], F32, name=name, tag=tag, align_bytes=64)
            lcols = slice(first * P // LIST_ROWS, (first + count) * P // LIST_ROWS)
            for t in range(PACK):
                src = ga[:, t, :].indirect(entries[:, lcols])
                if on_scalar:
                    nc.scalar.activation(out=picked[:, t, :], in_=src, func=ACT.Copy)
                else:
                    nc.vector.tensor_copy(out=picked[:, t, :], in_=src)
            return [picked[:, :, i * P:(i + 1) * P] for i in range(count)]

        def clamp(c, pa, pb):
            lo = keep.tile([P, PACK, P], F32, name="lo%d" % c, tag="z_scales%d" % (c - 1) if c else "lo0", align_bytes=64)
            hi = keep.tile([P, PACK, P], F32, name="hi%d" % c, tag="zg%d" % (c - 1) if c else "hi0", align_bytes=64)
            mid = keep.tile([P, PACK, P], F32, name="mid%d" % c, tag="mid%d" % c, align_bytes=64)
            nc.vector.tensor_tensor(out=hi[:], in0=pa, in1=pb, op=ALU.max)
            nc.vector.tensor_tensor(out=lo[:], in0=pa, in1=pb, op=ALU.min)
            nc.vector.tensor_tensor(out=mid[:], in0=hi[:], in1=ga[:, :, c * P:(c + 1) * P], op=ALU.min)
            return lo, mid

        def median(c, lo, mid):
            grouped = keep.tile([P, P, PACK], BF16, name="z_grouped%d" % c, tag="zg%d" % c, align_bytes=64)
            nc.vector.tensor_tensor(
                out=grouped[:].rearrange("p (c i) j -> p c j i", i=4),
                in0=lo[:].rearrange("p j (c i) -> p c j i", i=4),
                in1=mid[:].rearrange("p j (c i) -> p c j i", i=4),
                op=ALU.max,
            )
            return grouped

        def make_cv(c, grouped):
            codes = keep.tile([P, P], U32, name="z_codes%d" % c, tag="z_codes%d" % c, align_bytes=64)
            scales = keep.tile([P, P], U8, name="z_scales%d" % c, tag="z_scales%d" % c, align_bytes=64)
            quantize(codes[:], scales[:], grouped[:])
            acc = psum.tile([P, N], F32, name="chain", tag="chain%d" % (c % 2))
            product(acc[:], codes[:], scales[:], z2_codes[:], z2_scales[:])
            cv = keep.tile([P, N], F32, name="cv%d" % c)
            nc.vector.tensor_scalar(out=cv[:], in0=acc[:], scalar1=0.0625, scalar2=None, op0=ALU.mult)
            return cv

        def fetch(c, cv):
            slope, bias = sl_t[:, c:c + 1], bias_t[:, c:c + 1]
            sg2 = keep.tile([P, W], F32, name="sg2_%d" % c)
            pa2 = keep.tile([P, W], F32, name="pa2_%d" % c)
            sg = keep.tile([P, W], F32, name="sg_%d" % c)
            pb2 = keep.tile([P, W], F32, name="pb2_%d" % c)
            nc.scalar.activation(out=sg2[:], in_=cv[:].indirect(n4_t[:]), func=ACT.Sigmoid, bias=bias, scale=slope)
            nc.scalar.activation(out=pa2[:], in_=cv[:].indirect(n3_t[:]), func=ACT.Copy)
            nc.scalar.activation(out=sg[:], in_=cv[:].indirect(n3_t[:]), func=ACT.Sigmoid, bias=bias, scale=slope)
            nc.scalar.activation(out=pb2[:], in_=cv[:].indirect(n4_t[:]), func=ACT.Copy)
            return sg2, pa2, sg, pb2

        def combine(name, tag, left, right, op):
            tile = keep.tile([P, W], F32, name=name, tag=tag, align_bytes=64)
            nc.vector.tensor_tensor(out=tile[:], in0=left[:], in1=right[:], op=op)
            return tile

        def put_back(c, ra, rb):
            rows = keep.tile([P, N], F32, name="rows%d" % c)
            nc.scalar.activation(out=rows[:].indirect(n3_t[:]), in_=ra[:], func=ACT.Copy)
            nc.scalar.activation(out=rows[:].indirect(n4_t[:]), in_=rb[:], func=ACT.Copy)
            nc.sync.dma_start(out=out_0[c * P:(c + 1) * P, :], in_=rows[:])
            return rows

        out_words = out_1[0].rearrange("l n r -> l (n r)").bitcast(I32)
        out_scales = keep.tile([P, CHUNKS, P], U8, name="out_scales", align_bytes=64)

        def make_planes(c, rows):
            turned = psum.tile([P, N], F32, name="turned", tag="chain%d" % ((c + 1) % 2))
            for nb in range(N // P):
                cols = slice(nb * P, (nb + 1) * P)
                nc.tensor.transpose(turned[:, cols], rows[:, cols], identity[:])
            pairs = keep.tile([P, N], BF16, name="pairs%d" % c, tag="zg3" if c == 1 else "pairs%d" % c, align_bytes=64)
            nc.vector.tensor_copy(
                out=pairs[:].rearrange("p (u g e) -> p u g e", u=2, e=2),
                in_=turned[:].rearrange("p (g u e) -> p u g e", u=2, e=2),
            )
            back = psum.tile([P, 2, P], F32, name="back", tag="acc_b", bufs=2)
            for u in range(2):
                nc.tensor.transpose(back[:, u, :], pairs[:].bitcast(F32)[:, u * P:(u + 1) * P], identity[:])
            grouped = keep.tile([P, P * PACK], BF16, name="out_grouped%d" % c, align_bytes=64)
            nc.vector.tensor_copy(
                out=grouped[:].bitcast(F32).rearrange("p (n u) -> p n u", u=2), in_=back[:].rearrange("p u n -> p n u")
            )
            codes = keep.tile([P, P], U32, name="out_codes%d" % c, align_bytes=64)
            nc.vector.quantize_mx(out=codes[:].bitcast(FP8X4), scales=out_scales[:, c, :], in_=grouped[:])
            for nb in range(N // P):
                nc.sync.dma_start(
                    out=out_words[QUAD * c:QUAD * (c + 1), nb * P:(nb + 1) * P],
                    in_=codes[QUAD * nb:QUAD * (nb + 1), :].bitcast(I32),
                )

        pa = look_up("pa0", "pa0", n1_t, 0, 1, True)
        pb = look_up("pb0", "pb0", n2_t, 0, 1, True)
        cv = make_cv(0, median(0, *clamp(0, pa[0], pb[0])))
        pa.extend(look_up("pa12", "xa_words", n1_t, 1, 2, True))
        pb.extend(look_up("pb12", "xa_scales", n2_t, 1, 2, True))
        rows = []
        for c in range(CHUNKS):
            last = c == CHUNKS - 1
            sg2, pa2, sg, pb2 = fetch(c, cv)
            if c == CHUNKS - 2:
                pa.extend(look_up("pa3", "z_scales0", n1_t, 3, 1, False))
                pb.extend(look_up("pb3", "z_scales1", n2_t, 3, 1, False))
            if not last:
                lo, mid = clamp(c + 1, pa[c + 1], pb[c + 1])
            ra = combine("ra%d" % c, "ra_last" if last else "zg%d" % c, pa2, sg2, ALU.mult)
            if not last:
                grouped = median(c + 1, lo, mid)
            rb = combine("rb%d" % c, "rb_last" if last else "mid%d" % (c + 1), pb2, sg, ALU.subtract)
            rows.append(put_back(c, ra, rb))
            if not last:
                cv = make_cv(c + 1, grouped)
        for c in range(CHUNKS):
            make_planes(c, rows[c])
        for nb in range(N // P):
            nc.scalar.dma_start(
                out=out_2[0][:, nb * P:(nb + 1) * P].bitcast(I32).rearrange("(c r) w -> r c w", r=4),
                in_=out_scales[QUAD * nb:QUAD * nb + 4, :, :].bitcast(I32),
            )
